import numpy as np
import ml_dtypes


def mxq(x, axis, fmt="e4m3"):
    dtype, down = {"e4m3": (ml_dtypes.float8_e4m3fn, 7), "e5m2": (ml_dtypes.float8_e5m2, 14)}[fmt]
    v = np.moveaxis(np.asarray(x, np.float32).astype(ml_dtypes.bfloat16).astype(np.float64), axis, -1)
    blocks = v.reshape(v.shape[:-1] + (-1, 32))
    amax = np.abs(blocks).max(-1, keepdims=True)
    byte = np.maximum(np.where(amax > 0, np.frexp(amax)[1] - 1 + 127, 0) - down, 1)
    scale = np.exp2(byte - 127.0)
    codes = (blocks / scale).astype(np.float32).astype(dtype).astype(np.float64)
    return np.moveaxis((codes * scale).reshape(v.shape), -1, axis)


WIDE = False


def mx_kscale(k):
    if not WIDE:
        return np.ones(k)
    levels = np.array([10, -10, 5, -5, 0])
    if k % 512:
        return np.exp2(np.random.permutation(np.resize(levels, k // 32))).repeat(32)
    a = np.empty((k // 512, 16))
    for p in range(k // 512):
        a[p, :8] = np.random.permutation(np.resize(levels, 8))
        for g in range(8):
            far = levels[np.abs(levels - a[p, g]) >= 10]
            a[p, g + 8] = far[np.random.randint(len(far))]
    return np.exp2(a.ravel()).repeat(32)


def f64(x):
    return np.asarray(x).astype(np.float64)


def striped(idx):
    return np.tile(np.asarray(idx).reshape(-1, 16).T, (8, 1)).astype(np.uint16)


def unstriped(offs):
    return offs[:16].T.reshape(-1).astype(np.int64)


E2M1 = np.array([0.0, 0.5, 1.0, 1.5, 2.0, 3.0, 4.0, 6.0, -0.0, -0.5, -1.0, -1.5, -2.0, -3.0, -4.0, -6.0])


def pack_weight(w, fmt):
    k, n = w.shape
    w = f64(np.asarray(w, np.float32).astype(ml_dtypes.bfloat16)).reshape(k // 32, 32, n)
    amax = np.abs(w).max(1)
    if fmt == "e4m3":
        byte = np.frexp(amax)[1] - 1 + 127 - 7
    else:
        mant, ex = np.frexp(amax / 6.0)
        byte = np.where(mant > 0.5, ex, ex - 1) + 127
    byte = np.clip(np.where(amax > 0, byte, 1), 1, 254)
    scaled = (w * np.exp2(127.0 - byte)[:, None, :]).reshape(k, n).astype(np.float32)
    by_word = np.ascontiguousarray(scaled.reshape(k // 512, 128, 4, n).transpose(0, 1, 3, 2))
    if fmt == "e4m3":
        words = by_word.astype(ml_dtypes.float8_e4m3fn).view(np.uint8)
    else:
        c = by_word.astype(ml_dtypes.float4_e2m1fn).view(np.uint8) & 0xF
        words = (c[..., 0::2] | (c[..., 1::2] << 4)).reshape(k // 512, 128, 2 * n)
    return np.ascontiguousarray(words), np.ascontiguousarray(byte.astype(np.uint8).reshape(k // 512, 16, n))


def unpack_weight(words, scales, fmt):
    g, _, n = scales.shape
    words = np.ascontiguousarray(words).reshape(g, 128, n, -1)
    if fmt == "e4m3":
        vals = words.view(ml_dtypes.float8_e4m3fn).astype(np.float64)
    else:
        nib = np.empty((g, 128, n, 4), np.uint8)
        nib[..., 0::2] = words & 0xF
        nib[..., 1::2] = words >> 4
        vals = E2M1[nib]
    vals = vals * np.repeat(np.exp2(scales.astype(np.float64) - 127.0), 8, axis=1)[..., None]
    return vals.transpose(0, 1, 3, 2).reshape(g * 512, n)


D, T, V, I, Q = 512, 4096, 2048, 512, 128


def setup_inputs():
    n = np.random.standard_normal
    idx = np.random.permutation(T)[:V]
    idx2 = np.random.permutation(V)[:I]
    fd = mx_kscale(D)
    vocp = pack_weight(n((D, T)) / fd[:, None], "e4m3")
    return {
        "hid": (n((D, Q)) * 1.0 / np.sqrt(D) * fd[:, None]).astype(np.float32),
        "voc_words": vocp[0],
        "voc_scales": vocp[1],
        "fore": (np.random.uniform(0.1, 1.0, (Q, I))).astype(np.float32),
        "back": (np.random.uniform(0.1, 1.0, (Q, I))).astype(np.float32),
        "offs": striped(idx),
        "offs2": striped(idx2),
    }


def reference(hid, voc_words, voc_scales, fore, back, offs, offs2):
    idx = unstriped(offs)
    idx2 = unstriped(offs2)
    vocu = unpack_weight(voc_words, voc_scales, "e4m3")
    hidq = mxq(f64(hid), 0, "e4m3")
    vocidxg = vocu[:, idx]
    a = hidq.T @ vocidxg
    p = np.exp(a - np.max(a, axis=1, keepdims=True))
    g = f64(fore) * f64(back)
    gn = g / np.sum(g, axis=1, keepdims=True)
    gf = np.zeros((Q, V))
    gf[:, idx2] = gn
    y = (p / np.sum(p, axis=1, keepdims=True) - gf) * 2048.0
    return y

@@ -1,0 +1,131 @@
+from contextlib import ExitStack
+
+import concourse.mybir as mybir
+
+D, T, V, I, Q = 512, 4096, 2048, 512, 128
+FLOPS = 2 * D * V * Q
+
+F32 = mybir.dt.float32
+BF16 = mybir.dt.bfloat16
+I32 = mybir.dt.int32
+U32 = mybir.dt.uint32
+U16 = mybir.dt.uint16
+U8 = mybir.dt.uint8
+FP8X4 = mybir.dt.float8_e4m3fn_x4
+ALU = mybir.AluOpType
+ACT = mybir.ActivationFunctionType
+AXIS = mybir.AxisListType
+
+P = 128
+PACK = 4
+CHUNK = 512
+CHUNKS = V // CHUNK
+GROUP = 16
+OUT_SCALE = 2048.0
+
+
+def tile_attend_glabels_kernel(tc, hid, voc_words, voc_scales, fore, back, offs, offs2, out):
+    nc = tc.nc
+    with ExitStack() as ctx:
+        sb = ctx.enter_context(tc.tile_pool(name="sb", bufs=1))
+        ps = ctx.enter_context(tc.psum_pool(name="ps", bufs=1))
+
+        offsets = sb.tile([P, V // GROUP], U16, name="offsets")
+        offsets2 = sb.tile([P, I // GROUP], U16, name="offsets2")
+        scale_pool = sb.tile([P, T], U8, name="scale_pool", align_bytes=64)
+        placed = sb.tile([P, V], F32, name="placed")
+        fore_sb = sb.tile([P, I], F32, name="fore_sb")
+        back_sb = sb.tile([P, I], F32, name="back_sb")
+        hid_sb = sb.tile([P, PACK, Q], F32, name="hid_sb", tag="staged", align_bytes=64)
+
+        nc.vector.memset(scale_pool[:].bitcast(I32), 0)
+        nc.vector.memset(placed[:], 0.0)
+
+        nc.sync.dma_start(offsets[:], offs)
+        for quad in range(4):
+            nc.sync.dma_start(
+                scale_pool[32 * quad : 32 * quad + 4, :].bitcast(I32),
+                voc_scales[0, 4 * quad : 4 * quad + 4, :].bitcast(I32),
+            )
+        nc.scalar.dma_start(hid_sb[:], hid.rearrange("(p j) q -> p j q", j=PACK))
+        nc.scalar.dma_start(fore_sb[:], fore)
+        nc.scalar.dma_start(back_sb[:], back)
+        nc.sync.dma_start(offsets2[:], offs2)
+
+        hid_bf = sb.tile([P, Q, PACK], BF16, name="hid_bf", align_bytes=64)
+        nc.scalar.copy(hid_bf[:], hid_sb[:].rearrange("p j q -> p q j"))
+        word_pool = sb.tile([P, T], I32, name="word_pool", tag="staged", align_bytes=64)
+        nc.sync.dma_start(word_pool[:], voc_words[0].rearrange("p n t -> p (n t)").bitcast(I32))
+
+        voc_scale = sb.tile([P, V], U8, name="voc_scale", align_bytes=64)
+        nc.vector.tensor_copy(voc_scale[:], scale_pool[:].indirect(offsets[:]))
+
+        prod = sb.tile([P, I], F32, name="prod")
+        prod_part = sb.tile([P, I], F32, name="prod_part")
+        prod_sum = sb.tile([P, 1], F32, name="prod_sum")
+        prod_inv = sb.tile([P, 1], F32, name="prod_inv")
+        minus_one = sb.tile([P, 1], F32, name="minus_one")
+        quot = sb.tile([P, I], F32, name="quot")
+        nc.gpsimd.memset(minus_one[:], -1.0)
+        nc.gpsimd.tensor_tensor(prod[:], fore_sb[:], back_sb[:], ALU.mult)
+        nc.scalar.activation(prod_part[:], prod[:], ACT.Copy, scale=1.0 / OUT_SCALE, accum_out=prod_sum[:])
+        nc.gpsimd.tensor_tensor(prod_inv[:], prod_sum[:], minus_one[:], ALU.pow)
+        nc.scalar.activation(quot[:], prod[:], ACT.Copy, scale=prod_inv[:])
+
+        hid_codes = sb.tile([P, Q], U32, name="hid_codes", align_bytes=64)
+        hid_scale = sb.tile([P, Q], U8, name="hid_scale", align_bytes=64)
+        nc.vector.quantize_mx(
+            out=hid_codes[:].bitcast(FP8X4), scales=hid_scale[:], in_=hid_bf[:].rearrange("p q j -> p (q j)")
+        )
+
+        nc.vector.tensor_copy(placed[:].indirect(offsets2[:]), quot[:])
+
+        neg_max = sb.tile([P, CHUNKS], F32, name="neg_max")
+        sums = sb.tile([P, CHUNKS], F32, name="sums")
+        probs = []
+        for c in range(CHUNKS):
+            cols = slice(c * CHUNK, (c + 1) * CHUNK)
+            words = sb.tile([P, CHUNK], U32, name="words%d" % c, align_bytes=64)
+            nc.vector.tensor_copy(
+                words[:],
+                word_pool[:].bitcast(U32).indirect(offsets[:, c * CHUNK // GROUP : (c + 1) * CHUNK // GROUP]),
+            )
+            scores = ps.tile([P, CHUNK], F32, name="scores%d" % c)
+            nc.tensor.matmul_mx(
+                out=scores[:],
+                lhsT=hid_codes[:].bitcast(FP8X4),
+                lhsT_scale=hid_scale[:],
+                rhs=words[:].bitcast(FP8X4),
+                rhs_scale=voc_scale[:, cols],
+                start=True,
+                stop=True,
+            )
+            nc.vector.tensor_reduce(neg_max[:, c : c + 1], scores[:], AXIS.X, ALU.max, negate=True)
+            prob = sb.tile([P, CHUNK], F32, name="prob%d" % c)
+            nc.scalar.activation(
+                prob[:], scores[:], ACT.Exp, bias=neg_max[:, c : c + 1], accum_out=sums[:, c : c + 1]
+            )
+            probs.append(prob)
+
+        neg_top = sb.tile([P, 1], F32, name="neg_top")
+        shift = sb.tile([P, CHUNKS], F32, name="shift")
+        weighted = sb.tile([P, CHUNKS], F32, name="weighted")
+        total = sb.tile([P, 1], F32, name="total")
+        inv_total = sb.tile([P, 1], F32, name="inv_total")
+        factor = sb.tile([P, CHUNKS], F32, name="factor")
+        nc.vector.tensor_reduce(neg_top[:], neg_max[:], AXIS.X, ALU.min)
+        nc.scalar.activation(shift[:], neg_max[:], ACT.Exp, bias=neg_top[:], scale=-1.0)
+        nc.vector.scalar_tensor_tensor(
+            weighted[:], shift[:], 1.0 / OUT_SCALE, sums[:], ALU.mult, ALU.mult, accum_out=total[:]
+        )
+        nc.vector.reciprocal(inv_total[:], total[:])
+        nc.vector.tensor_scalar(factor[:], shift[:], inv_total[:], None, ALU.mult)
+
+        for c in range(CHUNKS):
+            cols = slice(c * CHUNK, (c + 1) * CHUNK)
+            res = sb.tile([P, CHUNK], F32, name="res%d" % c)
+            nc.vector.scalar_tensor_tensor(
+                res[:], probs[c][:], factor[:, c : c + 1], placed[:, cols], ALU.mult, ALU.subtract
+            )
+            queue = nc.sync if c % 2 == 0 else nc.scalar
+            queue.dma_start(out[:, cols], res[:])

@@ -20,6 +20,7 @@ P = 128
 PACK = 4
 CHUNK = 512
 CHUNKS = V // CHUNK
+PIECE = 256
 GROUP = 16
 OUT_SCALE = 2048.0
 
@@ -34,13 +35,25 @@ def tile_attend_glabels_kernel(tc, hid, voc_words, voc_scales, fore, back, offs,
         offsets2 = sb.tile([P, I // GROUP], U16, name="offsets2")
         scale_pool = sb.tile([P, T], U8, name="scale_pool", align_bytes=64)
         placed = sb.tile([P, V], F32, name="placed")
-        fore_sb = sb.tile([P, I], F32, name="fore_sb")
-        back_sb = sb.tile([P, I], F32, name="back_sb")
         hid_sb = sb.tile([P, PACK, Q], F32, name="hid_sb", tag="staged", align_bytes=64)
 
-        nc.vector.memset(scale_pool[:].bitcast(I32), 0)
+        nc.gpsimd.memset(scale_pool[:].bitcast(I32), 0)
         nc.vector.memset(placed[:], 0.0)
 
+        nc.sync.dma_start(offsets2[:], offs2)
+        half = I // 2
+        for h in range(2):
+            labels = slice(h * half, (h + 1) * half)
+            fore_sb = sb.tile([P, half], F32, name="fore%d" % h)
+            back_sb = sb.tile([P, half], F32, name="back%d" % h)
+            nc.sync.dma_start(fore_sb[:], fore[:, labels])
+            nc.scalar.dma_start(back_sb[:], back[:, labels])
+            nc.vector.tensor_tensor(
+                placed[:].indirect(offsets2[:, h * half // GROUP : (h + 1) * half // GROUP]),
+                fore_sb[:],
+                back_sb[:],
+                ALU.mult,
+            )
         nc.sync.dma_start(offsets[:], offs)
         for quad in range(4):
             nc.sync.dma_start(
@@ -48,29 +61,11 @@ def tile_attend_glabels_kernel(tc, hid, voc_words, voc_scales, fore, back, offs,
                 voc_scales[0, 4 * quad : 4 * quad + 4, :].bitcast(I32),
             )
         nc.scalar.dma_start(hid_sb[:], hid.rearrange("(p j) q -> p j q", j=PACK))
-        nc.scalar.dma_start(fore_sb[:], fore)
-        nc.scalar.dma_start(back_sb[:], back)
-        nc.sync.dma_start(offsets2[:], offs2)
 
         hid_bf = sb.tile([P, Q, PACK], BF16, name="hid_bf", align_bytes=64)
         nc.scalar.copy(hid_bf[:], hid_sb[:].rearrange("p j q -> p q j"))
         word_pool = sb.tile([P, T], I32, name="word_pool", tag="staged", align_bytes=64)
         nc.sync.dma_start(word_pool[:], voc_words[0].rearrange("p n t -> p (n t)").bitcast(I32))
-
-        voc_scale = sb.tile([P, V], U8, name="voc_scale", align_bytes=64)
-        nc.vector.tensor_copy(voc_scale[:], scale_pool[:].indirect(offsets[:]))
-
-        prod = sb.tile([P, I], F32, name="prod")
-        prod_part = sb.tile([P, I], F32, name="prod_part")
-        prod_sum = sb.tile([P, 1], F32, name="prod_sum")
-        prod_inv = sb.tile([P, 1], F32, name="prod_inv")
-        minus_one = sb.tile([P, 1], F32, name="minus_one")
-        quot = sb.tile([P, I], F32, name="quot")
-        nc.gpsimd.memset(minus_one[:], -1.0)
-        nc.gpsimd.tensor_tensor(prod[:], fore_sb[:], back_sb[:], ALU.mult)
-        nc.scalar.activation(prod_part[:], prod[:], ACT.Copy, scale=1.0 / OUT_SCALE, accum_out=prod_sum[:])
-        nc.gpsimd.tensor_tensor(prod_inv[:], prod_sum[:], minus_one[:], ALU.pow)
-        nc.scalar.activation(quot[:], prod[:], ACT.Copy, scale=prod_inv[:])
 
         hid_codes = sb.tile([P, Q], U32, name="hid_codes", align_bytes=64)
         hid_scale = sb.tile([P, Q], U8, name="hid_scale", align_bytes=64)
@@ -78,7 +73,17 @@ def tile_attend_glabels_kernel(tc, hid, voc_words, voc_scales, fore, back, offs,
             out=hid_codes[:].bitcast(FP8X4), scales=hid_scale[:], in_=hid_bf[:].rearrange("p q j -> p (q j)")
         )
 
-        nc.vector.tensor_copy(placed[:].indirect(offsets2[:]), quot[:])
+        voc_scale = sb.tile([P, V], U8, name="voc_scale", align_bytes=64)
+        nc.vector.tensor_copy(voc_scale[:], scale_pool[:].indirect(offsets[:]))
+
+        target = sb.tile([P, V], F32, name="target")
+        label_sum = sb.tile([P, 1], F32, name="label_sum")
+        label_inv = sb.tile([P, 1], F32, name="label_inv")
+        minus_one = sb.tile([P, 1], F32, name="minus_one")
+        nc.gpsimd.memset(minus_one[:], -1.0)
+        nc.scalar.activation(target[:], placed[:], ACT.Copy, scale=1.0 / OUT_SCALE, accum_out=label_sum[:])
+        nc.gpsimd.tensor_tensor(label_inv[:], label_sum[:], minus_one[:], ALU.pow)
+        nc.scalar.activation(target[:], placed[:], ACT.Copy, scale=label_inv[:])
 
         neg_max = sb.tile([P, CHUNKS], F32, name="neg_max")
         sums = sb.tile([P, CHUNKS], F32, name="sums")
@@ -112,20 +117,24 @@ def tile_attend_glabels_kernel(tc, hid, voc_words, voc_scales, fore, back, offs,
         weighted = sb.tile([P, CHUNKS], F32, name="weighted")
         total = sb.tile([P, 1], F32, name="total")
         inv_total = sb.tile([P, 1], F32, name="inv_total")
-        factor = sb.tile([P, CHUNKS], F32, name="factor")
         nc.vector.tensor_reduce(neg_top[:], neg_max[:], AXIS.X, ALU.min)
         nc.scalar.activation(shift[:], neg_max[:], ACT.Exp, bias=neg_top[:], scale=-1.0)
         nc.vector.scalar_tensor_tensor(
             weighted[:], shift[:], 1.0 / OUT_SCALE, sums[:], ALU.mult, ALU.mult, accum_out=total[:]
         )
         nc.vector.reciprocal(inv_total[:], total[:])
-        nc.vector.tensor_scalar(factor[:], shift[:], inv_total[:], None, ALU.mult)
 
         for c in range(CHUNKS):
-            cols = slice(c * CHUNK, (c + 1) * CHUNK)
-            res = sb.tile([P, CHUNK], F32, name="res%d" % c)
-            nc.vector.scalar_tensor_tensor(
-                res[:], probs[c][:], factor[:, c : c + 1], placed[:, cols], ALU.mult, ALU.subtract
-            )
-            queue = nc.sync if c % 2 == 0 else nc.scalar
-            queue.dma_start(out[:, cols], res[:])
+            nc.scalar.activation(probs[c][:], probs[c][:], ACT.Copy, scale=shift[:, c : c + 1])
+            for k in range(CHUNK // PIECE):
+                first = c * CHUNK + k * PIECE
+                res = sb.tile([P, PIECE], F32, name="res%d" % first)
+                nc.vector.scalar_tensor_tensor(
+                    res[:],
+                    probs[c][:, k * PIECE : (k + 1) * PIECE],
+                    inv_total[:],
+                    target[:, first : first + PIECE],
+                    ALU.mult,
+                    ALU.subtract,
+                )
+                nc.sync.dma_start(out[:, first : first + PIECE], res[:])

@@ -20,7 +20,8 @@ P = 128
 PACK = 4
 CHUNK = 512
 CHUNKS = V // CHUNK
-PIECE = 256
+GATHER = 1024
+CUTS = (0, 256, 512, 768, 1024, 1280, 1536, 1792, 2048)
 GROUP = 16
 OUT_SCALE = 2048.0
 
@@ -48,6 +49,8 @@ def tile_attend_glabels_kernel(tc, hid, voc_words, voc_scales, fore, back, offs,
             back_sb = sb.tile([P, half], F32, name="back%d" % h)
             nc.sync.dma_start(fore_sb[:], fore[:, labels])
             nc.scalar.dma_start(back_sb[:], back[:, labels])
+            if h == 0:
+                nc.scalar.dma_start(hid_sb[:], hid.rearrange("(p j) q -> p j q", j=PACK))
             nc.vector.tensor_tensor(
                 placed[:].indirect(offsets2[:, h * half // GROUP : (h + 1) * half // GROUP]),
                 fore_sb[:],
@@ -60,7 +63,6 @@ def tile_attend_glabels_kernel(tc, hid, voc_words, voc_scales, fore, back, offs,
                 scale_pool[32 * quad : 32 * quad + 4, :].bitcast(I32),
                 voc_scales[0, 4 * quad : 4 * quad + 4, :].bitcast(I32),
             )
-        nc.scalar.dma_start(hid_sb[:], hid.rearrange("(p j) q -> p j q", j=PACK))
 
         hid_bf = sb.tile([P, Q, PACK], BF16, name="hid_bf", align_bytes=64)
         nc.scalar.copy(hid_bf[:], hid_sb[:].rearrange("p j q -> p q j"))
@@ -87,30 +89,30 @@ def tile_attend_glabels_kernel(tc, hid, voc_words, voc_scales, fore, back, offs,
 
         neg_max = sb.tile([P, CHUNKS], F32, name="neg_max")
         sums = sb.tile([P, CHUNKS], F32, name="sums")
-        probs = []
-        for c in range(CHUNKS):
-            cols = slice(c * CHUNK, (c + 1) * CHUNK)
-            words = sb.tile([P, CHUNK], U32, name="words%d" % c, align_bytes=64)
+        prob = sb.tile([P, V], F32, name="prob")
+        for g in range(V // GATHER):
+            words = sb.tile([P, GATHER], U32, name="words%d" % g, align_bytes=64)
             nc.vector.tensor_copy(
                 words[:],
-                word_pool[:].bitcast(U32).indirect(offsets[:, c * CHUNK // GROUP : (c + 1) * CHUNK // GROUP]),
+                word_pool[:].bitcast(U32).indirect(offsets[:, g * GATHER // GROUP : (g + 1) * GATHER // GROUP]),
             )
-            scores = ps.tile([P, CHUNK], F32, name="scores%d" % c)
-            nc.tensor.matmul_mx(
-                out=scores[:],
-                lhsT=hid_codes[:].bitcast(FP8X4),
-                lhsT_scale=hid_scale[:],
-                rhs=words[:].bitcast(FP8X4),
-                rhs_scale=voc_scale[:, cols],
-                start=True,
-                stop=True,
-            )
-            nc.vector.tensor_reduce(neg_max[:, c : c + 1], scores[:], AXIS.X, ALU.max, negate=True)
-            prob = sb.tile([P, CHUNK], F32, name="prob%d" % c)
-            nc.scalar.activation(
-                prob[:], scores[:], ACT.Exp, bias=neg_max[:, c : c + 1], accum_out=sums[:, c : c + 1]
-            )
-            probs.append(prob)
+            for k in range(GATHER // CHUNK):
+                c = g * (GATHER // CHUNK) + k
+                cols = slice(c * CHUNK, (c + 1) * CHUNK)
+                scores = ps.tile([P, CHUNK], F32, name="scores%d" % c)
+                nc.tensor.matmul_mx(
+                    out=scores[:],
+                    lhsT=hid_codes[:].bitcast(FP8X4),
+                    lhsT_scale=hid_scale[:],
+                    rhs=words[:, k * CHUNK : (k + 1) * CHUNK].bitcast(FP8X4),
+                    rhs_scale=voc_scale[:, cols],
+                    start=True,
+                    stop=True,
+                )
+                nc.vector.tensor_reduce(neg_max[:, c : c + 1], scores[:], AXIS.X, ALU.max, negate=True)
+                nc.scalar.activation(
+                    prob[:, cols], scores[:], ACT.Exp, bias=neg_max[:, c : c + 1], accum_out=sums[:, c : c + 1]
+                )
 
         neg_top = sb.tile([P, 1], F32, name="neg_top")
         shift = sb.tile([P, CHUNKS], F32, name="shift")
@@ -124,17 +126,19 @@ def tile_attend_glabels_kernel(tc, hid, voc_words, voc_scales, fore, back, offs,
         )
         nc.vector.reciprocal(inv_total[:], total[:])
 
-        for c in range(CHUNKS):
-            nc.scalar.activation(probs[c][:], probs[c][:], ACT.Copy, scale=shift[:, c : c + 1])
-            for k in range(CHUNK // PIECE):
-                first = c * CHUNK + k * PIECE
-                res = sb.tile([P, PIECE], F32, name="res%d" % first)
-                nc.vector.scalar_tensor_tensor(
-                    res[:],
-                    probs[c][:, k * PIECE : (k + 1) * PIECE],
-                    inv_total[:],
-                    target[:, first : first + PIECE],
-                    ALU.mult,
-                    ALU.subtract,
-                )
-                nc.sync.dma_start(out[:, first : first + PIECE], res[:])
+        factor = sb.tile([P, CHUNKS], F32, name="factor")
+        nc.scalar.activation(prob[:, :CHUNK], prob[:, :CHUNK], ACT.Copy, scale=shift[:, 0:1])
+        nc.scalar.activation(factor[:], shift[:], ACT.Copy, scale=inv_total[:])
+        for first, last in zip(CUTS[:-1], CUTS[1:]):
+            cols = slice(first, last)
+            c = first // CHUNK
+            res = sb.tile([P, last - first], F32, name="res%d" % first)
+            nc.vector.scalar_tensor_tensor(
+                res[:],
+                prob[:, cols],
+                inv_total[:] if c == 0 else factor[:, c : c + 1],
+                target[:, cols],
+                ALU.mult,
+                ALU.subtract,
+            )
+            nc.sync.dma_start(out[:, cols], res[:])

@@ -20,8 +20,7 @@ P = 128
 PACK = 4
 CHUNK = 512
 CHUNKS = V // CHUNK
-GATHER = 1024
-CUTS = (0, 256, 512, 768, 1024, 1280, 1536, 1792, 2048)
+CUTS = (0, 256, 512, 1024, 1536, 2048)
 GROUP = 16
 OUT_SCALE = 2048.0
 
@@ -90,29 +89,36 @@ def tile_attend_glabels_kernel(tc, hid, voc_words, voc_scales, fore, back, offs,
         neg_max = sb.tile([P, CHUNKS], F32, name="neg_max")
         sums = sb.tile([P, CHUNKS], F32, name="sums")
         prob = sb.tile([P, V], F32, name="prob")
-        for g in range(V // GATHER):
-            words = sb.tile([P, GATHER], U32, name="words%d" % g, align_bytes=64)
+        def gather_words(c):
+            words = sb.tile([P, CHUNK], U32, name="words", tag="words", bufs=3, align_bytes=64)
             nc.vector.tensor_copy(
                 words[:],
-                word_pool[:].bitcast(U32).indirect(offsets[:, g * GATHER // GROUP : (g + 1) * GATHER // GROUP]),
+                word_pool[:].bitcast(U32).indirect(offsets[:, c * CHUNK // GROUP : (c + 1) * CHUNK // GROUP]),
             )
-            for k in range(GATHER // CHUNK):
-                c = g * (GATHER // CHUNK) + k
-                cols = slice(c * CHUNK, (c + 1) * CHUNK)
-                scores = ps.tile([P, CHUNK], F32, name="scores%d" % c)
-                nc.tensor.matmul_mx(
-                    out=scores[:],
-                    lhsT=hid_codes[:].bitcast(FP8X4),
-                    lhsT_scale=hid_scale[:],
-                    rhs=words[:, k * CHUNK : (k + 1) * CHUNK].bitcast(FP8X4),
-                    rhs_scale=voc_scale[:, cols],
-                    start=True,
-                    stop=True,
-                )
-                nc.vector.tensor_reduce(neg_max[:, c : c + 1], scores[:], AXIS.X, ALU.max, negate=True)
-                nc.scalar.activation(
-                    prob[:, cols], scores[:], ACT.Exp, bias=neg_max[:, c : c + 1], accum_out=sums[:, c : c + 1]
-                )
+            return words
+
+        def score_chunk(c, words):
+            cols = slice(c * CHUNK, (c + 1) * CHUNK)
+            scores = ps.tile([P, CHUNK], F32, name="scores%d" % c)
+            nc.tensor.matmul_mx(
+                out=scores[:],
+                lhsT=hid_codes[:].bitcast(FP8X4),
+                lhsT_scale=hid_scale[:],
+                rhs=words[:].bitcast(FP8X4),
+                rhs_scale=voc_scale[:, cols],
+                start=True,
+                stop=True,
+            )
+            nc.vector.tensor_reduce(neg_max[:, c : c + 1], scores[:], AXIS.X, ALU.max, negate=True)
+            nc.scalar.activation(
+                prob[:, cols], scores[:], ACT.Exp, bias=neg_max[:, c : c + 1], accum_out=sums[:, c : c + 1]
+            )
+
+        gathered = [gather_words(0), gather_words(1)]
+        for c in range(CHUNKS):
+            if c + 2 < CHUNKS:
+                gathered.append(gather_words(c + 2))
+            score_chunk(c, gathered[c])
 
         neg_top = sb.tile([P, 1], F32, name="neg_top")
         shift = sb.tile([P, CHUNKS], F32, name="shift")

from contextlib import ExitStack

import concourse.mybir as mybir

D, T, V, I, Q = 512, 4096, 2048, 512, 128
FLOPS = 2 * D * V * Q

F32 = mybir.dt.float32
BF16 = mybir.dt.bfloat16
I32 = mybir.dt.int32
U32 = mybir.dt.uint32
U16 = mybir.dt.uint16
U8 = mybir.dt.uint8
FP8X4 = mybir.dt.float8_e4m3fn_x4
ALU = mybir.AluOpType
ACT = mybir.ActivationFunctionType
AXIS = mybir.AxisListType

P = 128
PACK = 4
CHUNK = 512
CHUNKS = V // CHUNK
CUTS = (0, 256, 512, 1024, 1536, 2048)
GROUP = 16
OUT_SCALE = 2048.0


def tile_attend_glabels_kernel(tc, hid, voc_words, voc_scales, fore, back, offs, offs2, out):
    nc = tc.nc
    with ExitStack() as ctx:
        sb = ctx.enter_context(tc.tile_pool(name="sb", bufs=1))
        ps = ctx.enter_context(tc.psum_pool(name="ps", bufs=1))

        offsets = sb.tile([P, V // GROUP], U16, name="offsets")
        offsets2 = sb.tile([P, I // GROUP], U16, name="offsets2")
        scale_pool = sb.tile([P, T], U8, name="scale_pool", align_bytes=64)
        placed = sb.tile([P, V], F32, name="placed")
        hid_sb = sb.tile([P, PACK, Q], F32, name="hid_sb", tag="staged", align_bytes=64)

        nc.gpsimd.memset(scale_pool[:].bitcast(I32), 0)
        nc.vector.memset(placed[:], 0.0)

        nc.sync.dma_start(offsets2[:], offs2)
        half = I // 2
        for h in range(2):
            labels = slice(h * half, (h + 1) * half)
            fore_sb = sb.tile([P, half], F32, name="fore%d" % h)
            back_sb = sb.tile([P, half], F32, name="back%d" % h)
            nc.sync.dma_start(fore_sb[:], fore[:, labels])
            nc.scalar.dma_start(back_sb[:], back[:, labels])
            if h == 0:
                nc.scalar.dma_start(hid_sb[:], hid.rearrange("(p j) q -> p j q", j=PACK))
            nc.vector.tensor_tensor(
                placed[:].indirect(offsets2[:, h * half // GROUP : (h + 1) * half // GROUP]),
                fore_sb[:],
                back_sb[:],
                ALU.mult,
            )
        nc.sync.dma_start(offsets[:], offs)
        for quad in range(4):
            nc.sync.dma_start(
                scale_pool[32 * quad : 32 * quad + 4, :].bitcast(I32),
                voc_scales[0, 4 * quad : 4 * quad + 4, :].bitcast(I32),
            )

        hid_bf = sb.tile([P, Q, PACK], BF16, name="hid_bf", align_bytes=64)
        nc.scalar.copy(hid_bf[:], hid_sb[:].rearrange("p j q -> p q j"))
        word_pool = sb.tile([P, T], I32, name="word_pool", tag="staged", align_bytes=64)
        nc.sync.dma_start(word_pool[:], voc_words[0].rearrange("p n t -> p (n t)").bitcast(I32))

        hid_codes = sb.tile([P, Q], U32, name="hid_codes", align_bytes=64)
        hid_scale = sb.tile([P, Q], U8, name="hid_scale", align_bytes=64)
        nc.vector.quantize_mx(
            out=hid_codes[:].bitcast(FP8X4), scales=hid_scale[:], in_=hid_bf[:].rearrange("p q j -> p (q j)")
        )

        voc_scale = sb.tile([P, V], U8, name="voc_scale", align_bytes=64)
        nc.vector.tensor_copy(voc_scale[:], scale_pool[:].indirect(offsets[:]))

        target = sb.tile([P, V], F32, name="target")
        label_sum = sb.tile([P, 1], F32, name="label_sum")
        label_inv = sb.tile([P, 1], F32, name="label_inv")
        minus_one = sb.tile([P, 1], F32, name="minus_one")
        nc.gpsimd.memset(minus_one[:], -1.0)
        nc.scalar.activation(target[:], placed[:], ACT.Copy, scale=1.0 / OUT_SCALE, accum_out=label_sum[:])
        nc.gpsimd.tensor_tensor(label_inv[:], label_sum[:], minus_one[:], ALU.pow)
        nc.scalar.activation(target[:], placed[:], ACT.Copy, scale=label_inv[:])

        neg_max = sb.tile([P, CHUNKS], F32, name="neg_max")
        sums = sb.tile([P, CHUNKS], F32, name="sums")
        prob = sb.tile([P, V], F32, name="prob")
        def gather_words(c):
            words = sb.tile([P, CHUNK], U32, name="words", tag="words", bufs=3, align_bytes=64)
            nc.vector.tensor_copy(
                words[:],
                word_pool[:].bitcast(U32).indirect(offsets[:, c * CHUNK // GROUP : (c + 1) * CHUNK // GROUP]),
            )
            return words

        def score_chunk(c, words):
            cols = slice(c * CHUNK, (c + 1) * CHUNK)
            scores = ps.tile([P, CHUNK], F32, name="scores%d" % c)
            nc.tensor.matmul_mx(
                out=scores[:],
                lhsT=hid_codes[:].bitcast(FP8X4),
                lhsT_scale=hid_scale[:],
                rhs=words[:].bitcast(FP8X4),
                rhs_scale=voc_scale[:, cols],
                start=True,
                stop=True,
            )
            nc.vector.tensor_reduce(neg_max[:, c : c + 1], scores[:], AXIS.X, ALU.max, negate=True)
            nc.scalar.activation(
                prob[:, cols], scores[:], ACT.Exp, bias=neg_max[:, c : c + 1], accum_out=sums[:, c : c + 1]
            )

        gathered = [gather_words(0), gather_words(1)]
        for c in range(CHUNKS):
            if c + 2 < CHUNKS:
                gathered.append(gather_words(c + 2))
            score_chunk(c, gathered[c])

        neg_top = sb.tile([P, 1], F32, name="neg_top")
        shift = sb.tile([P, CHUNKS], F32, name="shift")
        weighted = sb.tile([P, CHUNKS], F32, name="weighted")
        total = sb.tile([P, 1], F32, name="total")
        inv_total = sb.tile([P, 1], F32, name="inv_total")
        nc.vector.tensor_reduce(neg_top[:], neg_max[:], AXIS.X, ALU.min)
        nc.scalar.activation(shift[:], neg_max[:], ACT.Exp, bias=neg_top[:], scale=-1.0)
        nc.vector.scalar_tensor_tensor(
            weighted[:], shift[:], 1.0 / OUT_SCALE, sums[:], ALU.mult, ALU.mult, accum_out=total[:]
        )
        nc.vector.reciprocal(inv_total[:], total[:])

        factor = sb.tile([P, CHUNKS], F32, name="factor")
        nc.scalar.activation(prob[:, :CHUNK], prob[:, :CHUNK], ACT.Copy, scale=shift[:, 0:1])
        nc.scalar.activation(factor[:], shift[:], ACT.Copy, scale=inv_total[:])
        for first, last in zip(CUTS[:-1], CUTS[1:]):
            cols = slice(first, last)
            c = first // CHUNK
            res = sb.tile([P, last - first], F32, name="res%d" % first)
            nc.vector.scalar_tensor_tensor(
                res[:],
                prob[:, cols],
                inv_total[:] if c == 0 else factor[:, c : c + 1],
                target[:, cols],
                ALU.mult,
                ALU.subtract,
            )
            nc.sync.dma_start(out[:, cols], res[:])
